import numpy as np
import ml_dtypes


def mxq(x, axis, fmt="e4m3"):
    dtype, down = {"e4m3": (ml_dtypes.float8_e4m3fn, 7), "e5m2": (ml_dtypes.float8_e5m2, 14)}[fmt]
    v = np.moveaxis(np.asarray(x, np.float32).astype(ml_dtypes.bfloat16).astype(np.float64), axis, -1)
    blocks = v.reshape(v.shape[:-1] + (-1, 32))
    amax = np.abs(blocks).max(-1, keepdims=True)
    byte = np.maximum(np.where(amax > 0, np.frexp(amax)[1] - 1 + 127, 0) - down, 1)
    scale = np.exp2(byte - 127.0)
    codes = (blocks / scale).astype(np.float32).astype(dtype).astype(np.float64)
    return np.moveaxis((codes * scale).reshape(v.shape), -1, axis)


WIDE = False


def mx_kscale(k):
    if not WIDE:
        return np.ones(k)
    levels = np.array([10, -10, 5, -5, 0])
    if k % 512:
        return np.exp2(np.random.permutation(np.resize(levels, k // 32))).repeat(32)
    a = np.empty((k // 512, 16))
    for p in range(k // 512):
        a[p, :8] = np.random.permutation(np.resize(levels, 8))
        for g in range(8):
            far = levels[np.abs(levels - a[p, g]) >= 10]
            a[p, g + 8] = far[np.random.randint(len(far))]
    return np.exp2(a.ravel()).repeat(32)


BF16 = ml_dtypes.bfloat16


def bf(x):
    return np.asarray(x, np.float32).astype(BF16)


def f64(x):
    return np.asarray(x).astype(np.float64)


E2M1 = np.array([0.0, 0.5, 1.0, 1.5, 2.0, 3.0, 4.0, 6.0, -0.0, -0.5, -1.0, -1.5, -2.0, -3.0, -4.0, -6.0])


def pack_weight(w, fmt):
    k, n = w.shape
    w = f64(bf(w)).reshape(k // 32, 32, n)
    amax = np.abs(w).max(1)
    if fmt == "e4m3":
        byte = np.frexp(amax)[1] - 1 + 127 - 7
    else:
        mant, ex = np.frexp(amax / 6.0)
        byte = np.where(mant > 0.5, ex, ex - 1) + 127
    byte = np.clip(np.where(amax > 0, byte, 1), 1, 254)
    scaled = (w * np.exp2(127.0 - byte)[:, None, :]).reshape(k, n).astype(np.float32)
    by_word = np.ascontiguousarray(scaled.reshape(k // 512, 128, 4, n).transpose(0, 1, 3, 2))
    if fmt == "e4m3":
        words = by_word.astype(ml_dtypes.float8_e4m3fn).view(np.uint8)
    else:
        c = by_word.astype(ml_dtypes.float4_e2m1fn).view(np.uint8) & 0xF
        words = c[..., 0::2] | (c[..., 1::2] << 4)
    return np.ascontiguousarray(words), np.ascontiguousarray(byte.astype(np.uint8).reshape(k // 512, 16, n))


def unpack_weight(words, scales, fmt):
    g, p, n, _ = words.shape
    if fmt == "e4m3":
        vals = np.ascontiguousarray(words).view(ml_dtypes.float8_e4m3fn).astype(np.float64)
    else:
        nib = np.empty((g, p, n, 4), np.uint8)
        nib[..., 0::2] = words & 0xF
        nib[..., 1::2] = words >> 4
        vals = E2M1[nib]
    vals = vals * np.repeat(np.exp2(scales.astype(np.float64) - 127.0), 8, axis=1)[..., None]
    return vals.transpose(0, 1, 3, 2).reshape(g * 512, n)
def pack4(w):
    words, scales = pack_weight(w, "e2m1")
    return words.reshape(words.shape[0], 128, -1), scales


def unpack4(words, scales):
    return unpack_weight(words.reshape(words.shape[0], 128, -1, 2), scales, "e2m1")


def planes(Y):
    n, m = Y.shape
    b = f64(bf(Y)).reshape(n // 32, 32, m)
    amax = np.abs(b).max(1)
    byte = np.clip(np.where(amax > 0, np.frexp(amax)[1] - 1 + 127 - 7, 1), 1, 254)
    codes = (b * np.exp2(127.0 - byte)[:, None, :]).reshape(n, m).astype(np.float32).astype(ml_dtypes.float8_e4m3fn).view(np.uint8)
    words = codes.reshape(n // 512, 128, 4, m).transpose(0, 1, 3, 2)
    return np.ascontiguousarray(words), np.ascontiguousarray(byte.astype(np.uint8).reshape(n // 512, 16, m))


T, D, N = 1024, 1024, 1024

ETA = 0.8
GAMMA_KEEP = 0.85
GAMMA_MIX = 0.15


def setup_inputs():
    s, t = mx_kscale(D), mx_kscale(D)[::-1]
    v = bf(np.random.standard_normal((T, D)) * s)
    pinv_words, pinv_scales = pack4(np.random.standard_normal((D, D)) / np.sqrt(D) / s[:, None])
    surp = bf(np.random.standard_normal(T))
    m = bf(np.random.standard_normal((T, D)) * 0.7)
    g = bf((1.0 + 0.1 * np.random.standard_normal(D)) * t)
    arms_words, arms_scales = pack4((np.random.standard_normal((N, D)) / np.sqrt(D) / t).T)
    return {
        "v": v,
        "pinv_words": pinv_words,
        "pinv_scales": pinv_scales,
        "surp": surp,
        "m": m,
        "g": g,
        "arms_words": arms_words,
        "arms_scales": arms_scales,
        "logw": bf(np.random.standard_normal((T, N)) * 0.5),
        "mu": bf(np.random.uniform(0.5, 2.5, N)),
    }


def estimate_loss(v, pinv, surp, m):
    z = mxq(v, 1, "e4m3") @ pinv
    return m + surp[:, None] * z


def over_mean(x):
    return x / np.mean(x, axis=-1, keepdims=True)


def core(v, pinv_words, pinv_scales, surp, m, g, arms_words, arms_scales, logw, mu):
    lhat = estimate_loss(f64(v), unpack4(pinv_words, pinv_scales), f64(surp), f64(m))
    u = lhat * f64(g)[None, :]
    s = mxq(u, 1, "e4m3") @ unpack4(arms_words, arms_scales)
    y = f64(logw) - ETA * s
    r = over_mean(np.exp(y))
    mu = f64(mu)
    q = GAMMA_KEEP * r + (GAMMA_MIX * mu / np.mean(mu))[None, :]
    return np.log(q)


def reference(v, pinv_words, pinv_scales, surp, m, g, arms_words, arms_scales, logw, mu):
    R_out = core(v, pinv_words, pinv_scales, surp, m, g, arms_words, arms_scales, logw, mu)
    words, scales = planes(R_out)
    return R_out, words, scales

@@ -1,0 +1,314 @@
+import math
+from contextlib import ExitStack
+
+import concourse.mybir as mybir
+from concourse.masks import make_identity
+
+F32 = mybir.dt.float32
+BF16 = mybir.dt.bfloat16
+I32 = mybir.dt.int32
+U32 = mybir.dt.uint32
+U8 = mybir.dt.uint8
+FP8X4 = mybir.dt.float8_e4m3fn_x4
+FP4X4 = mybir.dt.float4_e2m1fn_x4
+ALU = mybir.AluOpType
+ACT = mybir.ActivationFunctionType
+AX = mybir.AxisListType
+
+P = 128
+T, D, N = 1024, 1024, 1024
+ETA, KEEP, MIX = 0.8, 0.85, 0.15
+FLOPS = 2 * T * D * D + 2 * T * D * N
+NTILES = T // P
+SOFT = (0, 1, 2, 3, 4)
+ORDER = """
+VT:0 G: C: vc:0 M: vq:0 VT:1 Z:00 Z:01 z:00 z:01 vc:1 g:00 c: VT:2 g:01 vq:1 vc:2 Z:11 vq:2 Z:10 z:11 UT:0
+z:10 g:11 VT:3 uc:0 Z:20 vc:3 uq:0 g:10 Z:21 z:20 S:01 z:21 S:00 g:20 vq:3 y:01 UT:1 y:00 Z:30 g:21 uc:1 VT:4
+z:30 e8:0 Z:31 uq:1 g:30 UT:2 z:31 vc:4 S:10 mx:0 uc:2 vq:4 g:31 S:11 y:10 E:0 VT:5 uq:2 y:11 Z:41 vc:5 r:0
+UT:3 z:41 e8:1 S:21 q:0 g:41 VT:6 uc:3 S:20 y:21 vc:6 Z:40 mx:1 uq:3 E:1 y:20 VT:7 vq:6 S:30 vq:5 vc:7 S:31
+z:40 e8:2 Z:50 r:1 y:30 g:40 Z:51 y:31 Z:60 q:1 e8:3 UT:4 mx:2 vq:7 uc:4 z:51 E:2 mx:3 uq:4 Z:70 g:51 z:50
+S:41 z:60 E:3 S:40 g:50 r:2 y:41 Z:71 q:2 Z:61 g:60 UT:5 z:61 l:1 z:71 g:61 r:3 z:70 uc:5 q:3 g:71 l:2 UT:6
+uq:5 g:70 y:40 uc:6 S:50 l:3 S:51 uq:6 y:50 S:60 y:51 l:0 UT:7 y:60 S:61 mx:5 uc:7 w:03 y:61 e8:4 uq:7 mx:6
+S:70 S:71 E:5 mx:4 y:70 y:71 E:6 r:5 oq:03 mx:7 E:4 q:5 E:7 r:4 r:6 w:02 q:4 oq:02 r:7 l:5 q:6 l:4 q:7 l:6
+w:00 w:01 l:72 oq:00 l:70 oq:01 so:0 l:71 w:12 l:73 w:11 oq:12 oq:11 w:13 w:10 oq:13 oq:10 so:1
+""".split()
+
+
+def tile_controlvariateexp2linearbanditpolicy_x2_kernel(
+    tc, v, pinv_words, pinv_scales, surp, m, g, arms_words, arms_scales, logw, mu, out_0, out_1, out_2
+):
+    nc = tc.nc
+    with ExitStack() as ctx:
+        keep = ctx.enter_context(tc.tile_pool(name="keep", bufs=1))
+        work = ctx.enter_context(tc.tile_pool(name="work", bufs=3))
+        psum = ctx.enter_context(tc.psum_pool(name="psum", bufs=1))
+        ctx.enter_context(tc.manual_schedule())
+
+        v_sb = [keep.tile([P, 4, D], BF16, name="v_sb%d" % i, align_bytes=64) for i in range(2)]
+        m_sb = [keep.tile([P, 4, D], BF16, name="m_sb%d" % i, align_bytes=64) for i in range(2)]
+        logw_sb = [keep.tile([P, 4, N], BF16, name="logw_sb%d" % i, align_bytes=64) for i in range(2)]
+        e_sb = [keep.tile([P, 4, N], F32, name="e_sb%d" % i, align_bytes=64) for i in range(2)]
+        o_sb = [keep.tile([P, 4, N], F32, name="o_sb%d" % i, align_bytes=64) for i in range(2)]
+        ocodes = [keep.tile([P, N], U32, name="ocodes%d" % i, align_bytes=64) for i in range(2)]
+        oscales = [keep.tile([P, N], U8, name="oscales%d" % i, align_bytes=64) for i in range(2)]
+        pw = keep.tile([P, 2, 2 * D], U8, name="pw", align_bytes=64)
+        aw = keep.tile([P, 2, 2 * N], U8, name="aw", align_bytes=64)
+        ps = keep.tile([P, 2 * D], U8, name="ps", align_bytes=64)
+        asc = keep.tile([P, 2 * N], U8, name="asc", align_bytes=64)
+        surp_sb = keep.tile([P, NTILES], F32, name="surp_sb")
+        rows = keep.tile([P, D], BF16, name="rows", align_bytes=64)
+        ident = keep.tile([P, P], F32, name="ident", align_bytes=64)
+        ident_bf = keep.tile([P, P], BF16, name="ident_bf", align_bytes=64)
+        g_all = keep.tile([P, D], BF16, name="g_all", align_bytes=64)
+        c_all = keep.tile([P, N], F32, name="c_all", align_bytes=64)
+        mu_sum = keep.tile([P, 2], F32, name="mu_sum")
+        mu_rec = keep.tile([P, 1], F32, name="mu_rec")
+        warm = keep.tile([P, 1], F32, name="warm")
+        esum = [keep.tile([P, 1], F32, name="esum%d" % i) for i in range(NTILES)]
+        erec = [keep.tile([P, 1], F32, name="erec%d" % i) for i in range(NTILES)]
+        shift = [keep.tile([P, 1], F32, name="shift%d" % i) for i in range(NTILES)]
+        soft = [keep.tile([P, 1], F32, name="soft%d" % i) for i in range(NTILES)]
+
+        def load_scales(dst, src):
+            for q in range(4):
+                nc.sync.dma_start(
+                    out=dst[32 * q : 32 * q + 4, :].bitcast(I32).rearrange("r (b n) -> r b n", b=2),
+                    in_=src[:, 4 * q : 4 * q + 4, :].rearrange("b r n -> r b n").bitcast(I32),
+                )
+
+        def load_words(dst, src):
+            nc.sync.dma_start(out=dst[:].bitcast(I32), in_=src.rearrange("b p n -> p b n").bitcast(I32))
+
+        def load_tile(dst, src, i):
+            rows_of = src[512 * (i // 4) : 512 * (i // 4) + 512, :].rearrange("(p t) d -> p t d", t=4)
+            nc.sync.dma_start(out=dst[i // 4][:, i % 4, :], in_=rows_of[:, i % 4, :])
+
+        nc.vector.memset(rows[:], 0.0)
+        for r, src in enumerate((g, surp, mu)):
+            nc.scalar.dma_start(out=rows[r : r + 1, :], in_=src.rearrange("(o d) -> o d", o=1))
+        nc.scalar.activation(out=warm[:], in_=warm_src(nc, keep), func=ACT.Exp)
+        nc.vector.memset(ps[:].bitcast(I32), 0)
+        nc.vector.memset(asc[:].bitcast(I32), 0)
+        make_identity(nc, ident[:])
+        nc.vector.tensor_copy(out=ident_bf[:], in_=ident[:])
+        load_tile(v_sb, v, 0)
+        load_words(pw, pinv_words)
+        load_scales(ps, pinv_scales)
+        load_tile(v_sb, v, 1)
+        load_tile(m_sb, m, 0)
+        load_tile(v_sb, v, 2)
+        load_tile(m_sb, m, 1)
+        load_tile(m_sb, m, 2)
+        load_words(aw, arms_words)
+        load_scales(asc, arms_scales)
+        load_tile(logw_sb, logw, 0)
+        load_tile(v_sb, v, 3)
+        load_tile(m_sb, m, 3)
+        load_tile(logw_sb, logw, 1)
+        for i in range(2, NTILES):
+            if i > 3:
+                load_tile(v_sb, v, i)
+                load_tile(m_sb, m, i)
+            load_tile(logw_sb, logw, i)
+
+        def spread(row, h, tag):
+            bank = psum.tile([P, 512], F32, name=tag, tag=tag, bufs=3)
+            nc.tensor.matmul(
+                bank[:], lhsT=ident_bf[:, row : row + 1].to_broadcast([P, P]), rhs=rows[:, 512 * h : 512 * h + 512],
+                start=True, stop=True,
+            )
+            return bank
+
+        def spread_g():
+            for h in range(2):
+                bank = spread(0, h, "z")
+                nc.scalar.copy(out=g_all[:, 512 * h : 512 * h + 512], in_=bank[:])
+
+        def surp_columns():
+            bank = psum.tile([P, 512], F32, name="s", tag="s", bufs=3)
+            for i in range(NTILES):
+                first = 512 * (i // 4) + i % 4
+                nc.tensor.matmul(
+                    bank[:, i : i + 1], lhsT=rows[:, first : first + 509 : 4], rhs=ident_bf[:, 1:2],
+                    start=True, stop=True,
+                )
+            nc.vector.tensor_copy(out=surp_sb[:], in_=bank[:, 0:NTILES])
+
+        def spread_mu():
+            for h in range(2):
+                bank = spread(2, h, "s")
+                nc.scalar.activation(
+                    out=c_all[:, 512 * h : 512 * h + 512], in_=bank[:], func=ACT.Identity,
+                    accum_out=mu_sum[:, h : h + 1],
+                )
+
+        def scale_mu():
+            nc.vector.tensor_add(out=mu_rec[:], in0=mu_sum[:, 0:1], in1=mu_sum[:, 1:2])
+            nc.vector.reciprocal(out=mu_rec[:], in_=mu_rec[:])
+            nc.vector.tensor_scalar(
+                out=c_all[:], in0=c_all[:], scalar1=mu_rec[:], scalar2=MIX / KEEP, op0=ALU.mult, op1=ALU.mult
+            )
+
+        live = {}
+
+        def transposes(src, bank):
+            words = src.bitcast(F32)
+            for b in range(2):
+                for u in range(2):
+                    nc.tensor.transpose(
+                        bank[:, b, u, :], words[:, 256 * b + u : 256 * (b + 1) : 2], ident[:]
+                    )
+
+        def words_out(bank, name):
+            kt = work.tile([P, 2 * P * 4], BF16, name=name, tag=name, align_bytes=64)
+            nc.scalar.copy(
+                out=kt[:].bitcast(F32).rearrange("p (b r u) -> p b r u", b=2, u=2),
+                in_=bank[:].rearrange("p b u r -> p b r u"),
+            )
+            return kt
+
+        def quantize(src, name, bufs):
+            codes = work.tile([P, 2 * P], U32, name=name + "c", tag=name + "c", bufs=bufs, align_bytes=64)
+            scales = work.tile([P, 2 * P], U8, name=name + "s", tag=name + "s", bufs=bufs, align_bytes=64)
+            nc.vector.quantize_mx(out=codes[:].bitcast(FP8X4), scales=scales[:], in_=src[:])
+            return codes, scales
+
+        def mx(bank, act, words, scales, h):
+            codes, act_scales = act
+            for b in range(2):
+                nc.tensor.matmul_mx(
+                    out=bank[:],
+                    lhsT=codes[:, P * b : P * b + P].bitcast(FP8X4),
+                    lhsT_scale=act_scales[:, P * b : P * b + P],
+                    rhs=words[:, b, 1024 * h : 1024 * h + 1024].bitcast(FP4X4),
+                    rhs_scale=scales[:, 1024 * b + 512 * h : 1024 * b + 512 * h + 512],
+                    start=(b == 0),
+                    stop=(b == 1),
+                )
+
+        def VT(i):
+            live["vtp", i] = bank = psum.tile([P, 2, 2, P], F32, name="vtp", tag="vtp", bufs=1)
+            transposes(v_sb[i // 4][:, i % 4, :], bank)
+
+        def vc(i):
+            live["vt", i] = words_out(live.pop(("vtp", i)), "vt")
+
+        def vq(i):
+            live["vx", i] = quantize(live.pop(("vt", i)), "vx", 5)
+
+        def Z(i, h):
+            live["z", i, h] = bank = psum.tile([P, 512], F32, name="z", tag="z", bufs=3)
+            mx(bank, live["vx", i], pw, ps, h)
+
+        def z(i, h):
+            if ("lh", i) not in live:
+                live["lh", i] = work.tile([P, D], F32, name="lh", tag="lh", bufs=4, align_bytes=64)
+            cols = slice(512 * h, 512 * h + 512)
+            nc.vector.scalar_tensor_tensor(
+                out=live["lh", i][:, cols], in0=live.pop(("z", i, h))[:], scalar=surp_sb[:, i : i + 1],
+                in1=m_sb[i // 4][:, i % 4, cols], op0=ALU.mult, op1=ALU.add,
+            )
+
+        def gm(i, h):
+            if ("u", i) not in live:
+                live["u", i] = work.tile([P, D], BF16, name="u", tag="u", bufs=4, align_bytes=64)
+            cols = slice(512 * h, 512 * h + 512)
+            nc.gpsimd.tensor_tensor(
+                out=live["u", i][:, cols], in0=live["lh", i][:, cols], in1=g_all[:, cols], op=ALU.mult
+            )
+
+        def UT(i):
+            live["utp", i] = bank = psum.tile([P, 2, 2, P], F32, name="utp", tag="utp", bufs=1)
+            transposes(live.pop(("u", i))[:], bank)
+
+        def uc(i):
+            live["ut", i] = words_out(live.pop(("utp", i)), "ut")
+
+        def uq(i):
+            live["ux", i] = quantize(live.pop(("ut", i)), "ux", 4)
+
+        def S(i, h):
+            live["s", i, h] = bank = psum.tile([P, 512], F32, name="s", tag="s", bufs=3)
+            mx(bank, live["ux", i], aw, asc, h)
+
+        def y(i, h):
+            if ("y", i) not in live:
+                live["y", i] = work.tile([P, N], F32, name="y", tag="y", bufs=5, align_bytes=64)
+            cols = slice(512 * h, 512 * h + 512)
+            nc.vector.scalar_tensor_tensor(
+                out=live["y", i][:, cols], in0=live.pop(("s", i, h))[:], scalar=ETA,
+                in1=logw_sb[i // 4][:, i % 4, cols], op0=ALU.mult, op1=ALU.subtract,
+            )
+
+        def e8(i):
+            junk = work.tile([P, N], BF16, name="junk", tag="junk", bufs=2, align_bytes=64)
+            nc.scalar.activation(out=junk[:], in_=live["y", i][:], func=ACT.Exp, scale=-0.125, accum_out=soft[i][:])
+
+        def mx_(i):
+            if i in SOFT:
+                nc.vector.tensor_scalar(
+                    out=shift[i][:], in0=soft[i][:].bitcast(I32), scalar1=-8.0 * math.log(2.0) / 2.0**23,
+                    scalar2=8.0 * 127.0 * math.log(2.0), op0=ALU.mult, op1=ALU.add,
+                )
+            else:
+                nc.vector.tensor_reduce(out=shift[i][:], in_=live["y", i][:], axis=AX.X, op=ALU.min)
+
+        def E(i):
+            nc.scalar.activation(
+                out=e_sb[i // 4][:, i % 4, :], in_=live.pop(("y", i))[:], func=ACT.Exp, scale=-1.0,
+                bias=shift[i][:], accum_out=esum[i][:],
+            )
+
+        def r(i):
+            nc.vector.reciprocal(out=erec[i][:], in_=esum[i][:])
+
+        def q(i):
+            nc.vector.scalar_tensor_tensor(
+                out=e_sb[i // 4][:, i % 4, :], in0=e_sb[i // 4][:, i % 4, :], scalar=erec[i][:], in1=c_all[:],
+                op0=ALU.mult, op1=ALU.add,
+            )
+
+        def ln(i, cols):
+            b, t = i // 4, i % 4
+            nc.scalar.activation(out=o_sb[b][:, t, cols], in_=e_sb[b][:, t, cols], func=ACT.Ln, scale=KEEP * N)
+            nc.sync.dma_start(
+                out=out_0[512 * b : 512 * b + 512, cols].rearrange("(p t) n -> p t n", t=4)[:, t, :],
+                in_=o_sb[b][:, t, cols],
+            )
+
+        def l(i, c=None):
+            ln(i, slice(0, N) if c is None else slice(256 * c, 256 * c + 256))
+
+        def w(b, c):
+            cols = slice(256 * c, 256 * c + 256)
+            live["ob", b, c] = ob = work.tile([P, 256, 4], BF16, name="ob", tag="ob", bufs=4, align_bytes=64)
+            nc.vector.tensor_copy(out=ob[:], in_=o_sb[b][:, :, cols].rearrange("p t n -> p n t"))
+
+        def oq(b, c):
+            cols = slice(256 * c, 256 * c + 256)
+            nc.vector.quantize_mx(
+                out=ocodes[b][:, cols].bitcast(FP8X4), scales=oscales[b][:, cols],
+                in_=live.pop(("ob", b, c))[:].rearrange("p n t -> p (n t)"),
+            )
+            nc.sync.dma_start(
+                out=out_1[b].rearrange("p n t -> p (n t)").bitcast(I32)[:, cols], in_=ocodes[b][:, cols].bitcast(I32)
+            )
+
+        def so(b):
+            for r in range(4):
+                nc.sync.dma_start(
+                    out=out_2[b][4 * r : 4 * r + 4, :].bitcast(I32), in_=oscales[b][32 * r : 32 * r + 4, :].bitcast(I32)
+                )
+
+        stages = {"VT": VT, "vc": vc, "vq": vq, "Z": Z, "z": z, "g": gm, "UT": UT, "uc": uc, "uq": uq, "S": S, "y": y,
+                  "e8": e8, "mx": mx_, "E": E, "q": q, "r": r, "l": l, "C": surp_columns, "w": w, "oq": oq, "so": so,
+                  "G": spread_g, "M": spread_mu, "c": scale_mu}
+        for token in ORDER:
+            name, digits = token.split(":")
+            stages[name](*[int(x) for x in digits])
+
+
+def warm_src(nc, keep):
+    one = keep.tile([P, 1], F32, name="one")
+    nc.vector.memset(one[:], 1.0)
+    return one[:]

@@ -20,17 +20,18 @@ T, D, N = 1024, 1024, 1024
 ETA, KEEP, MIX = 0.8, 0.85, 0.15
 FLOPS = 2 * T * D * D + 2 * T * D * N
 NTILES = T // P
-SOFT = (0, 1, 2, 3, 4)
+SOFT = (0, 1, 2, 3)
+NZ, NS, KV, GW = 2, 3, (), ("w00", "w01", "w02", "w03")
 ORDER = """
-VT:0 G: C: vc:0 M: vq:0 VT:1 Z:00 Z:01 z:00 z:01 vc:1 g:00 c: VT:2 g:01 vq:1 vc:2 Z:11 vq:2 Z:10 z:11 UT:0
-z:10 g:11 VT:3 uc:0 Z:20 vc:3 uq:0 g:10 Z:21 z:20 S:01 z:21 S:00 g:20 vq:3 y:01 UT:1 y:00 Z:30 g:21 uc:1 VT:4
-z:30 e8:0 Z:31 uq:1 g:30 UT:2 z:31 vc:4 S:10 mx:0 uc:2 vq:4 g:31 S:11 y:10 E:0 VT:5 uq:2 y:11 Z:41 vc:5 r:0
-UT:3 z:41 e8:1 S:21 q:0 g:41 VT:6 uc:3 S:20 y:21 vc:6 Z:40 mx:1 uq:3 E:1 y:20 VT:7 vq:6 S:30 vq:5 vc:7 S:31
-z:40 e8:2 Z:50 r:1 y:30 g:40 Z:51 y:31 Z:60 q:1 e8:3 UT:4 mx:2 vq:7 uc:4 z:51 E:2 mx:3 uq:4 Z:70 g:51 z:50
-S:41 z:60 E:3 S:40 g:50 r:2 y:41 Z:71 q:2 Z:61 g:60 UT:5 z:61 l:1 z:71 g:61 r:3 z:70 uc:5 q:3 g:71 l:2 UT:6
-uq:5 g:70 y:40 uc:6 S:50 l:3 S:51 uq:6 y:50 S:60 y:51 l:0 UT:7 y:60 S:61 mx:5 uc:7 w:03 y:61 e8:4 uq:7 mx:6
-S:70 S:71 E:5 mx:4 y:70 y:71 E:6 r:5 oq:03 mx:7 E:4 q:5 E:7 r:4 r:6 w:02 q:4 oq:02 r:7 l:5 q:6 l:4 q:7 l:6
-w:00 w:01 l:72 oq:00 l:70 oq:01 so:0 l:71 w:12 l:73 w:11 oq:12 oq:11 w:13 w:10 oq:13 oq:10 so:1
+VT:0 M: vc:0 G: vq:0 VT:1 Z:01 vc:1 c: Z:00 k:01 VT:2 vq:1 k:00 U:01 vc:2 Z:11 u:01 U:00 k:11 vq:2 Z:10 u:00
+Z:21 k:10 uq:0 VT:3 k:21 U:10 vc:3 S:00 u:10 S:01 y:00 U:11 y:01 Z:20 vq:3 e8:0 u:11 Z:31 uq:1 U:21 k:31 mx:0
+S:11 E:0 u:21 VT:4 y:11 U:31 k:20 r:0 q:0 vc:4 S:10 Z:30 y:10 U:20 k:30 u:31 VT:5 e8:1 vq:4 u:20 Z:40 uq:2
+vc:5 Z:41 mx:1 S:21 E:1 vq:5 S:20 y:21 U:30 k:41 y:20 k:40 r:1 VT:6 u:30 e8:2 U:41 q:1 U:40 vc:6 uq:3 Z:51
+u:41 S:31 mx:2 u:40 k:51 S:30 vq:6 E:2 y:31 VT:7 y:30 Z:61 vc:7 uq:4 Z:50 r:2 k:61 q:2 S:40 e8:3 S:41 y:40
+U:51 k:50 vq:7 mx:3 y:41 Z:71 E:3 u:51 Z:60 mx:4 U:50 k:71 k:60 U:61 u:50 Z:70 r:3 uq:5 q:3 U:60 S:50 l:1 u:61
+S:51 y:50 U:71 k:70 y:51 l:2 u:60 mx:5 U:70 l:3 uq:6 u:70 l:0 S:61 u:71 S:60 y:61 w:03 y:60 uq:7 w:02 mx:6 E:4
+S:71 S:70 y:71 w:01 E:5 y:70 oq:03 w:00 E:6 mx:7 oq:01 E:7 oq:00 oq:02 so:0 r:5 r:6 r:4 q:5 q:4 l:5 r:7 q:6
+l:4 q:7 l:6 l:71 l:72 w:11 l:70 l:73 w:12 oq:11 w:13 w:10 oq:13 oq:10 oq:12 so:1
 """.split()
 
 
@@ -55,11 +56,10 @@ def tile_controlvariateexp2linearbanditpolicy_x2_kernel(
         aw = keep.tile([P, 2, 2 * N], U8, name="aw", align_bytes=64)
         ps = keep.tile([P, 2 * D], U8, name="ps", align_bytes=64)
         asc = keep.tile([P, 2 * N], U8, name="asc", align_bytes=64)
-        surp_sb = keep.tile([P, NTILES], F32, name="surp_sb")
+        cols = keep.tile([P, 2, NTILES], F32, name="cols")
         rows = keep.tile([P, D], BF16, name="rows", align_bytes=64)
         ident = keep.tile([P, P], F32, name="ident", align_bytes=64)
         ident_bf = keep.tile([P, P], BF16, name="ident_bf", align_bytes=64)
-        g_all = keep.tile([P, D], BF16, name="g_all", align_bytes=64)
         c_all = keep.tile([P, N], F32, name="c_all", align_bytes=64)
         mu_sum = keep.tile([P, 2], F32, name="mu_sum")
         mu_rec = keep.tile([P, 1], F32, name="mu_rec")
@@ -112,27 +112,22 @@ def tile_controlvariateexp2linearbanditpolicy_x2_kernel(
             load_tile(logw_sb, logw, i)
 
         def spread(row, h, tag):
-            bank = psum.tile([P, 512], F32, name=tag, tag=tag, bufs=3)
+            bank = psum.tile([P, 512], F32, name=tag, tag=tag, bufs=NS)
             nc.tensor.matmul(
                 bank[:], lhsT=ident_bf[:, row : row + 1].to_broadcast([P, P]), rhs=rows[:, 512 * h : 512 * h + 512],
                 start=True, stop=True,
             )
             return bank
 
-        def spread_g():
-            for h in range(2):
-                bank = spread(0, h, "z")
-                nc.scalar.copy(out=g_all[:, 512 * h : 512 * h + 512], in_=bank[:])
-
-        def surp_columns():
-            bank = psum.tile([P, 512], F32, name="s", tag="s", bufs=3)
+        def columns():
+            bank = psum.tile([P, 512], F32, name="s", tag="s", bufs=NS)
             for i in range(NTILES):
                 first = 512 * (i // 4) + i % 4
                 nc.tensor.matmul(
-                    bank[:, i : i + 1], lhsT=rows[:, first : first + 509 : 4], rhs=ident_bf[:, 1:2],
+                    bank[:, 2 * i : 2 * i + 2], lhsT=rows[:, first : first + 509 : 4], rhs=ident_bf[:, 0:2],
                     start=True, stop=True,
                 )
-            nc.vector.tensor_copy(out=surp_sb[:], in_=bank[:, 0:NTILES])
+            nc.vector.tensor_copy(out=cols[:], in_=bank[:, 0 : 2 * NTILES].rearrange("p (i r) -> p r i", r=2))
 
         def spread_mu():
             for h in range(2):
@@ -170,7 +165,7 @@ def tile_controlvariateexp2linearbanditpolicy_x2_kernel(
         def quantize(src, name, bufs):
             codes = work.tile([P, 2 * P], U32, name=name + "c", tag=name + "c", bufs=bufs, align_bytes=64)
             scales = work.tile([P, 2 * P], U8, name=name + "s", tag=name + "s", bufs=bufs, align_bytes=64)
-            nc.vector.quantize_mx(out=codes[:].bitcast(FP8X4), scales=scales[:], in_=src[:])
+            nc.vector.quantize_mx(out=codes[:].bitcast(FP8X4), scales=scales[:], in_=src)
             return codes, scales
 
         def mx(bank, act, words, scales, h):
@@ -194,41 +189,48 @@ def tile_controlvariateexp2linearbanditpolicy_x2_kernel(
             live["vt", i] = words_out(live.pop(("vtp", i)), "vt")
 
         def vq(i):
-            live["vx", i] = quantize(live.pop(("vt", i)), "vx", 5)
+            live["vx", i] = quantize(live.pop(("vt", i))[:], "vx", 5)
 
         def Z(i, h):
-            live["z", i, h] = bank = psum.tile([P, 512], F32, name="z", tag="z", bufs=3)
+            live["z", i, h] = bank = psum.tile([P, 512], F32, name="z", tag="z", bufs=NZ)
             mx(bank, live["vx", i], pw, ps, h)
 
-        def z(i, h):
-            if ("lh", i) not in live:
-                live["lh", i] = work.tile([P, D], F32, name="lh", tag="lh", bufs=4, align_bytes=64)
-            cols = slice(512 * h, 512 * h + 512)
-            nc.vector.scalar_tensor_tensor(
-                out=live["lh", i][:, cols], in0=live.pop(("z", i, h))[:], scalar=surp_sb[:, i : i + 1],
-                in1=m_sb[i // 4][:, i % 4, cols], op0=ALU.mult, op1=ALU.add,
+        def k(i, h):
+            if ("k", i) not in live:
+                live["k", i] = work.tile([P, 2, 4, P], F32, name="kw", tag="kw", bufs=3, align_bytes=64)
+            src = live.pop(("z", i, h))[:].rearrange("p (j t) -> p t j", t=4)
+            if (i, h) in KV:
+                nc.vector.tensor_scalar_mul(out=live["k", i][:, h, :, :], in0=src, scalar1=cols[:, 1, i : i + 1])
+            else:
+                nc.scalar.activation(
+                    out=live["k", i][:, h, :, :], in_=src, func=ACT.Copy, scale=cols[:, 1, i : i + 1]
+                )
+
+        def U(i, h):
+            live["U", i, h] = bank = psum.tile([P, 4, P], F32, name="u", tag="u", bufs=2)
+            for t in range(4):
+                nc.tensor.matmul(
+                    bank[:, t, :], lhsT=m_sb[i // 4][:, i % 4, 512 * h + t : 512 * h + t + 509 : 4], rhs=ident_bf[:],
+                    start=True, stop=False,
+                )
+                nc.tensor.matmul(
+                    bank[:, t, :], lhsT=live["k", i][:, h, t, :], rhs=ident[:], is_transpose=True,
+                    start=False, stop=True,
+                )
+
+        def u(i, h):
+            if ("ut", i) not in live:
+                live["ut", i] = work.tile([P, 2, P, 4], BF16, name="ut", tag="ut", align_bytes=64)
+            nc.vector.tensor_tensor(
+                out=live["ut", i][:, h, :, :], in0=live.pop(("U", i, h))[:].rearrange("p t r -> p r t"),
+                in1=cols[:, 0:1, 4 * h : 4 * h + 4].to_broadcast([P, P, 4]), op=ALU.mult,
             )
-
-        def gm(i, h):
-            if ("u", i) not in live:
-                live["u", i] = work.tile([P, D], BF16, name="u", tag="u", bufs=4, align_bytes=64)
-            cols = slice(512 * h, 512 * h + 512)
-            nc.gpsimd.tensor_tensor(
-                out=live["u", i][:, cols], in0=live["lh", i][:, cols], in1=g_all[:, cols], op=ALU.mult
-            )
-
-        def UT(i):
-            live["utp", i] = bank = psum.tile([P, 2, 2, P], F32, name="utp", tag="utp", bufs=1)
-            transposes(live.pop(("u", i))[:], bank)
-
-        def uc(i):
-            live["ut", i] = words_out(live.pop(("utp", i)), "ut")
 
         def uq(i):
-            live["ux", i] = quantize(live.pop(("ut", i)), "ux", 4)
+            live["ux", i] = quantize(live.pop(("ut", i))[:].rearrange("p b r t -> p (b r t)"), "ux", 4)
 
         def S(i, h):
-            live["s", i, h] = bank = psum.tile([P, 512], F32, name="s", tag="s", bufs=3)
+            live["s", i, h] = bank = psum.tile([P, 512], F32, name="s", tag="s", bufs=NS)
             mx(bank, live["ux", i], aw, asc, h)
 
         def y(i, h):
@@ -280,9 +282,13 @@ def tile_controlvariateexp2linearbanditpolicy_x2_kernel(
             ln(i, slice(0, N) if c is None else slice(256 * c, 256 * c + 256))
 
         def w(b, c):
-            cols = slice(256 * c, 256 * c + 256)
+            ncols = slice(256 * c, 256 * c + 256)
             live["ob", b, c] = ob = work.tile([P, 256, 4], BF16, name="ob", tag="ob", bufs=4, align_bytes=64)
-            nc.vector.tensor_copy(out=ob[:], in_=o_sb[b][:, :, cols].rearrange("p t n -> p n t"))
+            src = o_sb[b][:, :, ncols].rearrange("p t n -> p n t")
+            if "w%d%d" % (b, c) in GW:
+                nc.gpsimd.tensor_scalar(out=ob[:], in0=src, scalar1=1.0, scalar2=0.0, op0=ALU.mult, op1=ALU.add)
+            else:
+                nc.vector.tensor_copy(out=ob[:], in_=src)
 
         def oq(b, c):
             cols = slice(256 * c, 256 * c + 256)
@@ -300,9 +306,9 @@ def tile_controlvariateexp2linearbanditpolicy_x2_kernel(
                     out=out_2[b][4 * r : 4 * r + 4, :].bitcast(I32), in_=oscales[b][32 * r : 32 * r + 4, :].bitcast(I32)
                 )
 
-        stages = {"VT": VT, "vc": vc, "vq": vq, "Z": Z, "z": z, "g": gm, "UT": UT, "uc": uc, "uq": uq, "S": S, "y": y,
-                  "e8": e8, "mx": mx_, "E": E, "q": q, "r": r, "l": l, "C": surp_columns, "w": w, "oq": oq, "so": so,
-                  "G": spread_g, "M": spread_mu, "c": scale_mu}
+        stages = {"VT": VT, "vc": vc, "vq": vq, "Z": Z, "k": k, "U": U, "u": u, "uq": uq, "S": S, "y": y,
+                  "e8": e8, "mx": mx_, "E": E, "q": q, "r": r, "l": l, "w": w, "oq": oq, "so": so,
+                  "G": columns, "M": spread_mu, "c": scale_mu}
         for token in ORDER:
             name, digits = token.split(":")
             stages[name](*[int(x) for x in digits])

@@ -21,17 +21,17 @@ ETA, KEEP, MIX = 0.8, 0.85, 0.15
 FLOPS = 2 * T * D * D + 2 * T * D * N
 NTILES = T // P
 SOFT = (0, 1, 2, 3)
-NZ, NS, KV, GW = 2, 3, (), ("w00", "w01", "w02", "w03")
+MODE, NVT, NU, NZ, NS, GW, SW = "EEBBBBBB", 1, 2, 3, 2, (), ()
 ORDER = """
-VT:0 M: vc:0 G: vq:0 VT:1 Z:01 vc:1 c: Z:00 k:01 VT:2 vq:1 k:00 U:01 vc:2 Z:11 u:01 U:00 k:11 vq:2 Z:10 u:00
-Z:21 k:10 uq:0 VT:3 k:21 U:10 vc:3 S:00 u:10 S:01 y:00 U:11 y:01 Z:20 vq:3 e8:0 u:11 Z:31 uq:1 U:21 k:31 mx:0
-S:11 E:0 u:21 VT:4 y:11 U:31 k:20 r:0 q:0 vc:4 S:10 Z:30 y:10 U:20 k:30 u:31 VT:5 e8:1 vq:4 u:20 Z:40 uq:2
-vc:5 Z:41 mx:1 S:21 E:1 vq:5 S:20 y:21 U:30 k:41 y:20 k:40 r:1 VT:6 u:30 e8:2 U:41 q:1 U:40 vc:6 uq:3 Z:51
-u:41 S:31 mx:2 u:40 k:51 S:30 vq:6 E:2 y:31 VT:7 y:30 Z:61 vc:7 uq:4 Z:50 r:2 k:61 q:2 S:40 e8:3 S:41 y:40
-U:51 k:50 vq:7 mx:3 y:41 Z:71 E:3 u:51 Z:60 mx:4 U:50 k:71 k:60 U:61 u:50 Z:70 r:3 uq:5 q:3 U:60 S:50 l:1 u:61
-S:51 y:50 U:71 k:70 y:51 l:2 u:60 mx:5 U:70 l:3 uq:6 u:70 l:0 S:61 u:71 S:60 y:61 w:03 y:60 uq:7 w:02 mx:6 E:4
-S:71 S:70 y:71 w:01 E:5 y:70 oq:03 w:00 E:6 mx:7 oq:01 E:7 oq:00 oq:02 so:0 r:5 r:6 r:4 q:5 q:4 l:5 r:7 q:6
-l:4 q:7 l:6 l:71 l:72 w:11 l:70 l:73 w:12 oq:11 w:13 w:10 oq:13 oq:10 oq:12 so:1
+VT:0 C: vc:0 G: Cc: vq:0 VT:1 Gc: Z:01 vc:1 Z:00 z:01 M: vq:1 VT:2 z:00 Mc: U:01 Z:10 u:01 vc:2 U:00 z:10 Z:11
+u:00 VT:3 vq:2 uq:0 U:10 vc:3 z:11 Z:21 u:10 S:01 vq:3 VT:4 z:21 U:11 y:01 vc:4 S:00 g:21 u:11 Z:20 y:00 VT:5
+vq:4 Z:30 uq:1 e8:0 z:20 Z:40 c: S:11 vc:5 S:10 mx:0 g:20 z:30 Z:31 E:0 y:11 VT:6 g:30 y:10 Z:41 z:31 vc:6
+UT:2 r:0 e8:1 vq:5 g:31 q:0 VT:7 Z:50 uc:2 z:41 vc:7 UT:3 mx:1 vq:6 g:41 uq:2 E:1 z:40 Z:60 z:50 S:21 uc:3
+g:40 z:60 S:20 Z:51 r:1 y:21 g:50 Z:61 y:20 UT:4 z:51 g:60 e8:2 z:61 vq:7 g:51 uc:4 uq:3 mx:2 Z:71 uq:4 g:61
+E:2 S:31 q:1 S:30 Z:70 y:31 UT:5 r:2 y:30 UT:6 z:71 uc:5 S:41 q:2 e8:3 S:40 y:41 g:71 uc:6 mx:3 y:40 E:3 uq:5
+mx:4 S:51 S:50 r:3 z:70 y:51 g:70 y:50 l:0 mx:5 l:1 UT:7 uq:6 q:3 l:2 S:61 S:60 uc:7 y:61 l:3 y:60 uq:7 mx:6
+S:71 S:70 w:03 E:4 y:71 y:70 E:6 oq:03 mx:7 E:5 r:4 w:02 r:6 E:7 q:4 r:5 oq:02 q:5 r:7 q:6 l:4 q:7 l:5 w:01
+l:6 w:00 l:70 oq:01 l:71 oq:00 so:0 l:72 w:10 l:73 w:11 w:13 oq:11 oq:13 w:12 oq:10 oq:12 so:1
 """.split()
 
 
@@ -57,6 +57,7 @@ def tile_controlvariateexp2linearbanditpolicy_x2_kernel(
         ps = keep.tile([P, 2 * D], U8, name="ps", align_bytes=64)
         asc = keep.tile([P, 2 * N], U8, name="asc", align_bytes=64)
         cols = keep.tile([P, 2, NTILES], F32, name="cols")
+        g_all = keep.tile([P, D], BF16, name="g_all", align_bytes=64)
         rows = keep.tile([P, D], BF16, name="rows", align_bytes=64)
         ident = keep.tile([P, P], F32, name="ident", align_bytes=64)
         ident_bf = keep.tile([P, P], BF16, name="ident_bf", align_bytes=64)
@@ -76,8 +77,11 @@ def tile_controlvariateexp2linearbanditpolicy_x2_kernel(
                     in_=src[:, 4 * q : 4 * q + 4, :].rearrange("b r n -> r b n").bitcast(I32),
                 )
 
-        def load_words(dst, src):
-            nc.sync.dma_start(out=dst[:].bitcast(I32), in_=src.rearrange("b p n -> p b n").bitcast(I32))
+        def load_words(dst, src, h):
+            part = slice(D * h, D * h + D)
+            nc.sync.dma_start(
+                out=dst[:, :, part].bitcast(I32), in_=src.rearrange("b p n -> p b n")[:, :, part].bitcast(I32)
+            )
 
         def load_tile(dst, src, i):
             rows_of = src[512 * (i // 4) : 512 * (i // 4) + 512, :].rearrange("(p t) d -> p t d", t=4)
@@ -92,14 +96,16 @@ def tile_controlvariateexp2linearbanditpolicy_x2_kernel(
         make_identity(nc, ident[:])
         nc.vector.tensor_copy(out=ident_bf[:], in_=ident[:])
         load_tile(v_sb, v, 0)
-        load_words(pw, pinv_words)
+        load_words(pw, pinv_words, 0)
         load_scales(ps, pinv_scales)
         load_tile(v_sb, v, 1)
+        load_words(pw, pinv_words, 1)
         load_tile(m_sb, m, 0)
         load_tile(v_sb, v, 2)
         load_tile(m_sb, m, 1)
         load_tile(m_sb, m, 2)
-        load_words(aw, arms_words)
+        load_words(aw, arms_words, 0)
+        load_words(aw, arms_words, 1)
         load_scales(asc, arms_scales)
         load_tile(logw_sb, logw, 0)
         load_tile(v_sb, v, 3)
@@ -112,7 +118,7 @@ def tile_controlvariateexp2linearbanditpolicy_x2_kernel(
             load_tile(logw_sb, logw, i)
 
         def spread(row, h, tag):
-            bank = psum.tile([P, 512], F32, name=tag, tag=tag, bufs=NS)
+            bank = psum.tile([P, 512], F32, name=tag, tag=tag, bufs={"z": NZ, "s": NS}[tag])
             nc.tensor.matmul(
                 bank[:], lhsT=ident_bf[:, row : row + 1].to_broadcast([P, P]), rhs=rows[:, 512 * h : 512 * h + 512],
                 start=True, stop=True,
@@ -120,18 +126,33 @@ def tile_controlvariateexp2linearbanditpolicy_x2_kernel(
             return bank
 
         def columns():
-            bank = psum.tile([P, 512], F32, name="s", tag="s", bufs=NS)
+            live["cols"] = bank = psum.tile([P, 512], F32, name="s", tag="s", bufs=NS)
             for i in range(NTILES):
                 first = 512 * (i // 4) + i % 4
                 nc.tensor.matmul(
                     bank[:, 2 * i : 2 * i + 2], lhsT=rows[:, first : first + 509 : 4], rhs=ident_bf[:, 0:2],
                     start=True, stop=True,
                 )
+
+        def copy_columns():
+            bank = live.pop("cols")
             nc.vector.tensor_copy(out=cols[:], in_=bank[:, 0 : 2 * NTILES].rearrange("p (i r) -> p r i", r=2))
+
+        def spread_g():
+            for h in range(2):
+                live["g", h] = spread(0, h, "z")
+
+        def copy_g():
+            for h in range(2):
+                nc.vector.tensor_copy(out=g_all[:, 512 * h : 512 * h + 512], in_=live.pop(("g", h))[:])
 
         def spread_mu():
             for h in range(2):
-                bank = spread(2, h, "s")
+                live["mu", h] = spread(2, h, "s")
+
+        def copy_mu():
+            for h in range(2):
+                bank = live.pop(("mu", h))
                 nc.scalar.activation(
                     out=c_all[:, 512 * h : 512 * h + 512], in_=bank[:], func=ACT.Identity,
                     accum_out=mu_sum[:, h : h + 1],
@@ -182,7 +203,7 @@ def tile_controlvariateexp2linearbanditpolicy_x2_kernel(
                 )
 
         def VT(i):
-            live["vtp", i] = bank = psum.tile([P, 2, 2, P], F32, name="vtp", tag="vtp", bufs=1)
+            live["vtp", i] = bank = psum.tile([P, 2, 2, P], F32, name="vtp", tag="vtp", bufs=NVT)
             transposes(v_sb[i // 4][:, i % 4, :], bank)
 
         def vc(i):
@@ -195,39 +216,49 @@ def tile_controlvariateexp2linearbanditpolicy_x2_kernel(
             live["z", i, h] = bank = psum.tile([P, 512], F32, name="z", tag="z", bufs=NZ)
             mx(bank, live["vx", i], pw, ps, h)
 
-        def k(i, h):
-            if ("k", i) not in live:
-                live["k", i] = work.tile([P, 2, 4, P], F32, name="kw", tag="kw", bufs=3, align_bytes=64)
-            src = live.pop(("z", i, h))[:].rearrange("p (j t) -> p t j", t=4)
-            if (i, h) in KV:
-                nc.vector.tensor_scalar_mul(out=live["k", i][:, h, :, :], in0=src, scalar1=cols[:, 1, i : i + 1])
-            else:
-                nc.scalar.activation(
-                    out=live["k", i][:, h, :, :], in_=src, func=ACT.Copy, scale=cols[:, 1, i : i + 1]
-                )
+        def z(i, h):
+            if ("lh", i) not in live:
+                live["lh", i] = work.tile([P, 2, 512], F32, name="lh", tag="lh", bufs=5, align_bytes=64)
+            out, src = live["lh", i][:, h, :], live.pop(("z", i, h))[:]
+            other = m_sb[i // 4][:, i % 4, 512 * h : 512 * h + 512]
+            if MODE[i] == "E":
+                out = out.rearrange("p (t j) -> p t j", t=4)
+                src, other = (x.rearrange("p (j t) -> p t j", t=4) for x in (src, other))
+            nc.vector.scalar_tensor_tensor(
+                out=out, in0=src, scalar=cols[:, 1, i : i + 1], in1=other, op0=ALU.mult, op1=ALU.add
+            )
+
+        def gm(i, h):
+            if ("u", i) not in live:
+                live["u", i] = work.tile([P, D], BF16, name="u", tag="u", bufs=5, align_bytes=64)
+            part = slice(512 * h, 512 * h + 512)
+            nc.gpsimd.tensor_tensor(
+                out=live["u", i][:, part], in0=live["lh", i][:, h, :], in1=g_all[:, part], op=ALU.mult
+            )
+
+        def UT(i):
+            live["utp", i] = bank = psum.tile([P, 2, 2, P], F32, name="up", tag="up", bufs=NU)
+            transposes(live.pop(("u", i))[:], bank)
+
+        def uc(i):
+            live["ut", i] = words_out(live.pop(("utp", i)), "ut")
 
         def U(i, h):
-            live["U", i, h] = bank = psum.tile([P, 4, P], F32, name="u", tag="u", bufs=2)
+            live["U", i, h] = bank = psum.tile([P, 4, P], F32, name="up", tag="up", bufs=NU)
             for t in range(4):
-                nc.tensor.matmul(
-                    bank[:, t, :], lhsT=m_sb[i // 4][:, i % 4, 512 * h + t : 512 * h + t + 509 : 4], rhs=ident_bf[:],
-                    start=True, stop=False,
-                )
-                nc.tensor.matmul(
-                    bank[:, t, :], lhsT=live["k", i][:, h, t, :], rhs=ident[:], is_transpose=True,
-                    start=False, stop=True,
-                )
+                nc.tensor.transpose(bank[:, t, :], live["lh", i][:, h, P * t : P * t + P], ident[:])
 
         def u(i, h):
             if ("ut", i) not in live:
-                live["ut", i] = work.tile([P, 2, P, 4], BF16, name="ut", tag="ut", align_bytes=64)
+                live["ut", i] = work.tile([P, 2 * P * 4], BF16, name="ut", tag="ut", align_bytes=64)
             nc.vector.tensor_tensor(
-                out=live["ut", i][:, h, :, :], in0=live.pop(("U", i, h))[:].rearrange("p t r -> p r t"),
+                out=live["ut", i][:, 512 * h : 512 * h + 512].rearrange("p (r t) -> p r t", t=4),
+                in0=live.pop(("U", i, h))[:].rearrange("p t r -> p r t"),
                 in1=cols[:, 0:1, 4 * h : 4 * h + 4].to_broadcast([P, P, 4]), op=ALU.mult,
             )
 
         def uq(i):
-            live["ux", i] = quantize(live.pop(("ut", i))[:].rearrange("p b r t -> p (b r t)"), "ux", 4)
+            live["ux", i] = quantize(live.pop(("ut", i))[:], "ux", 4)
 
         def S(i, h):
             live["s", i, h] = bank = psum.tile([P, 512], F32, name="s", tag="s", bufs=NS)
@@ -235,7 +266,7 @@ def tile_controlvariateexp2linearbanditpolicy_x2_kernel(
 
         def y(i, h):
             if ("y", i) not in live:
-                live["y", i] = work.tile([P, N], F32, name="y", tag="y", bufs=5, align_bytes=64)
+                live["y", i] = work.tile([P, N], F32, name="y", tag="y", bufs=4, align_bytes=64)
             cols = slice(512 * h, 512 * h + 512)
             nc.vector.scalar_tensor_tensor(
                 out=live["y", i][:, cols], in0=live.pop(("s", i, h))[:], scalar=ETA,
@@ -287,6 +318,8 @@ def tile_controlvariateexp2linearbanditpolicy_x2_kernel(
             src = o_sb[b][:, :, ncols].rearrange("p t n -> p n t")
             if "w%d%d" % (b, c) in GW:
                 nc.gpsimd.tensor_scalar(out=ob[:], in0=src, scalar1=1.0, scalar2=0.0, op0=ALU.mult, op1=ALU.add)
+            elif "w%d%d" % (b, c) in SW:
+                nc.scalar.copy(out=ob[:], in_=src)
             else:
                 nc.vector.tensor_copy(out=ob[:], in_=src)
 
@@ -306,9 +339,9 @@ def tile_controlvariateexp2linearbanditpolicy_x2_kernel(
                     out=out_2[b][4 * r : 4 * r + 4, :].bitcast(I32), in_=oscales[b][32 * r : 32 * r + 4, :].bitcast(I32)
                 )
 
-        stages = {"VT": VT, "vc": vc, "vq": vq, "Z": Z, "k": k, "U": U, "u": u, "uq": uq, "S": S, "y": y,
+        stages = {"VT": VT, "vc": vc, "vq": vq, "Z": Z, "z": z, "g": gm, "UT": UT, "uc": uc, "U": U, "u": u, "uq": uq, "S": S, "y": y,
                   "e8": e8, "mx": mx_, "E": E, "q": q, "r": r, "l": l, "w": w, "oq": oq, "so": so,
-                  "G": columns, "M": spread_mu, "c": scale_mu}
+                  "G": spread_g, "Gc": copy_g, "C": columns, "Cc": copy_columns, "M": spread_mu, "Mc": copy_mu, "c": scale_mu}
         for token in ORDER:
             name, digits = token.split(":")
             stages[name](*[int(x) for x in digits])

@@ -20,18 +20,18 @@ T, D, N = 1024, 1024, 1024
 ETA, KEEP, MIX = 0.8, 0.85, 0.15
 FLOPS = 2 * T * D * D + 2 * T * D * N
 NTILES = T // P
-SOFT = (0, 1, 2, 3)
-MODE, NVT, NU, NZ, NS, GW, SW = "EEBBBBBB", 1, 2, 3, 2, (), ()
+SOFT = (0, 1, 2, 3, 4)
+MODE, NVT, NU, NZ, NS, GW, SW, GQ = "EE2B2B2B", 1, 2, 2, 3, ("w00", "w01"), ("w13",), ()
 ORDER = """
-VT:0 C: vc:0 G: Cc: vq:0 VT:1 Gc: Z:01 vc:1 Z:00 z:01 M: vq:1 VT:2 z:00 Mc: U:01 Z:10 u:01 vc:2 U:00 z:10 Z:11
-u:00 VT:3 vq:2 uq:0 U:10 vc:3 z:11 Z:21 u:10 S:01 vq:3 VT:4 z:21 U:11 y:01 vc:4 S:00 g:21 u:11 Z:20 y:00 VT:5
-vq:4 Z:30 uq:1 e8:0 z:20 Z:40 c: S:11 vc:5 S:10 mx:0 g:20 z:30 Z:31 E:0 y:11 VT:6 g:30 y:10 Z:41 z:31 vc:6
-UT:2 r:0 e8:1 vq:5 g:31 q:0 VT:7 Z:50 uc:2 z:41 vc:7 UT:3 mx:1 vq:6 g:41 uq:2 E:1 z:40 Z:60 z:50 S:21 uc:3
-g:40 z:60 S:20 Z:51 r:1 y:21 g:50 Z:61 y:20 UT:4 z:51 g:60 e8:2 z:61 vq:7 g:51 uc:4 uq:3 mx:2 Z:71 uq:4 g:61
-E:2 S:31 q:1 S:30 Z:70 y:31 UT:5 r:2 y:30 UT:6 z:71 uc:5 S:41 q:2 e8:3 S:40 y:41 g:71 uc:6 mx:3 y:40 E:3 uq:5
-mx:4 S:51 S:50 r:3 z:70 y:51 g:70 y:50 l:0 mx:5 l:1 UT:7 uq:6 q:3 l:2 S:61 S:60 uc:7 y:61 l:3 y:60 uq:7 mx:6
-S:71 S:70 w:03 E:4 y:71 y:70 E:6 oq:03 mx:7 E:5 r:4 w:02 r:6 E:7 q:4 r:5 oq:02 q:5 r:7 q:6 l:4 q:7 l:5 w:01
-l:6 w:00 l:70 oq:01 l:71 oq:00 so:0 l:72 w:10 l:73 w:11 w:13 oq:11 oq:13 w:12 oq:10 oq:12 so:1
+VT:0 C: vc:0 G: Cc: vq:0 VT:1 Gc: Z:00 vc:1 Z:01 z:00 M: z:01 VT:2 Mc: vq:1 U:00 U:01 u:00 Z:10 vc:2 Z:11 u:01
+z:10 VT:3 z:11 vc:3 U:10 uq:0 vq:2 U:11 u:10 S:00 u:11 Z:21 Z:20 vq:3 y:00 k:21 S:01 uq:1 k:20 VT:4 c: U:21
+vc:4 y:01 U:20 u:21 Z:30 e8:0 vq:4 S:10 u:20 Z:31 z:30 S:11 uq:2 z:31 g:30 VT:5 mx:0 S:20 y:10 vc:5 g:31 Z:41
+y:11 E:0 Z:40 y:20 S:21 vq:5 k:40 UT:3 q:0 k:41 VT:6 uc:3 U:40 y:21 vc:6 Z:50 uq:3 e8:1 u:40 U:41 z:50 e8:2
+S:31 vq:6 u:41 S:30 g:50 Z:51 mx:1 y:31 E:1 VT:7 uq:4 z:51 Z:60 vc:7 y:30 S:40 g:51 Z:61 k:60 mx:2 y:40 S:41
+e8:3 vq:7 U:60 q:1 k:61 UT:5 E:2 u:60 Z:70 Z:71 mx:3 y:41 uc:5 z:70 E:3 z:71 U:61 g:70 e8:4 a:0 u:61 g:71 b:0
+mx:4 uq:5 uq:6 UT:7 q:2 l:0 S:51 S:60 q:3 uc:7 S:50 l:2 y:60 uq:7 l:3 y:50 S:71 y:51 l:1 S:61 y:71 S:70 mx:5
+w:00 y:61 y:70 E:4 mx:6 w:01 E:5 mx:7 E:6 oq:00 E:7 oq:01 so:0 a:1 q:4 b:1 a:2 q:6 l:4 b:2 q:5 l:6 q:7 l:5
+l:71 l:73 l:70 w:11 l:72 w:13 w:10 w:12 oq:11 oq:13 oq:10 oq:12 so:1
 """.split()
 
 
@@ -65,8 +65,8 @@ def tile_controlvariateexp2linearbanditpolicy_x2_kernel(
         mu_sum = keep.tile([P, 2], F32, name="mu_sum")
         mu_rec = keep.tile([P, 1], F32, name="mu_rec")
         warm = keep.tile([P, 1], F32, name="warm")
-        esum = [keep.tile([P, 1], F32, name="esum%d" % i) for i in range(NTILES)]
-        erec = [keep.tile([P, 1], F32, name="erec%d" % i) for i in range(NTILES)]
+        esum = [keep.tile([P, 4], F32, name="esum%d" % i) for i in range(2)]
+        inv = [keep.tile([P, 4], F32, name="inv%d" % i) for i in range(2)]
         shift = [keep.tile([P, 1], F32, name="shift%d" % i) for i in range(NTILES)]
         soft = [keep.tile([P, 1], F32, name="soft%d" % i) for i in range(NTILES)]
 
@@ -228,6 +228,15 @@ def tile_controlvariateexp2linearbanditpolicy_x2_kernel(
                 out=out, in0=src, scalar=cols[:, 1, i : i + 1], in1=other, op0=ALU.mult, op1=ALU.add
             )
 
+        def k(i, h):
+            if ("lh", i) not in live:
+                live["lh", i] = work.tile([P, 2, 512], F32, name="lh", tag="lh", bufs=5, align_bytes=64)
+            nc.scalar.activation(
+                out=live["lh", i][:, h, :].rearrange("p (t j) -> p t j", t=4),
+                in_=live.pop(("z", i, h))[:].rearrange("p (j t) -> p t j", t=4), func=ACT.Copy,
+                scale=cols[:, 1, i : i + 1],
+            )
+
         def gm(i, h):
             if ("u", i) not in live:
                 live["u", i] = work.tile([P, D], BF16, name="u", tag="u", bufs=5, align_bytes=64)
@@ -246,7 +255,17 @@ def tile_controlvariateexp2linearbanditpolicy_x2_kernel(
         def U(i, h):
             live["U", i, h] = bank = psum.tile([P, 4, P], F32, name="up", tag="up", bufs=NU)
             for t in range(4):
-                nc.tensor.transpose(bank[:, t, :], live["lh", i][:, h, P * t : P * t + P], ident[:])
+                part = live["lh", i][:, h, P * t : P * t + P]
+                if MODE[i] == "E":
+                    nc.tensor.transpose(bank[:, t, :], part, ident[:])
+                else:
+                    nc.tensor.matmul(
+                        bank[:, t, :], lhsT=m_sb[i // 4][:, i % 4, 512 * h + t : 512 * h + t + 509 : 4],
+                        rhs=ident_bf[:], start=True, stop=False,
+                    )
+                    nc.tensor.matmul(
+                        bank[:, t, :], lhsT=part, rhs=ident[:], is_transpose=True, start=False, stop=True
+                    )
 
         def u(i, h):
             if ("ut", i) not in live:
@@ -289,21 +308,39 @@ def tile_controlvariateexp2linearbanditpolicy_x2_kernel(
         def E(i):
             nc.scalar.activation(
                 out=e_sb[i // 4][:, i % 4, :], in_=live.pop(("y", i))[:], func=ACT.Exp, scale=-1.0,
-                bias=shift[i][:], accum_out=esum[i][:],
+                bias=shift[i][:], accum_out=esum[i // 4][:, i % 4 : i % 4 + 1],
             )
 
-        def r(i):
-            nc.vector.reciprocal(out=erec[i][:], in_=esum[i][:])
+        RANGES = [(0, slice(0, 4)), (1, slice(0, 3)), (1, slice(3, 4))]
+
+        def a(k):
+            b, part = RANGES[k]
+            nc.vector.tensor_scalar_mul(out=inv[b][:, part], in0=esum[b][:, part], scalar1=1.0 / (KEEP * N))
+
+        def b_(k):
+            b, part = RANGES[k]
+            nc.vector.reciprocal(out=inv[b][:, part], in_=inv[b][:, part])
+
+        def Q(i):
+            live["cs", i] = cs = work.tile([P, N], F32, name="cs", tag="cs", bufs=1, align_bytes=64)
+            nc.gpsimd.tensor_scalar(
+                out=cs[:], in0=c_all[:], scalar1=esum[i // 4][:, i % 4 : i % 4 + 1], scalar2=0.0, op0=ALU.mult,
+                op1=ALU.add,
+            )
 
         def q(i):
-            nc.vector.scalar_tensor_tensor(
-                out=e_sb[i // 4][:, i % 4, :], in0=e_sb[i // 4][:, i % 4, :], scalar=erec[i][:], in1=c_all[:],
-                op0=ALU.mult, op1=ALU.add,
-            )
+            e = e_sb[i // 4][:, i % 4, :]
+            if i in GQ:
+                nc.gpsimd.tensor_tensor(out=e, in0=e, in1=live.pop(("cs", i))[:], op=ALU.add)
+            else:
+                nc.vector.scalar_tensor_tensor(
+                    out=e, in0=c_all[:], scalar=esum[i // 4][:, i % 4 : i % 4 + 1], in1=e, op0=ALU.mult, op1=ALU.add
+                )
 
         def ln(i, cols):
             b, t = i // 4, i % 4
-            nc.scalar.activation(out=o_sb[b][:, t, cols], in_=e_sb[b][:, t, cols], func=ACT.Ln, scale=KEEP * N)
+            nc.scalar.activation(out=o_sb[b][:, t, cols], in_=e_sb[b][:, t, cols], func=ACT.Ln,
+                scale=inv[b][:, t : t + 1])
             nc.sync.dma_start(
                 out=out_0[512 * b : 512 * b + 512, cols].rearrange("(p t) n -> p t n", t=4)[:, t, :],
                 in_=o_sb[b][:, t, cols],
@@ -313,8 +350,11 @@ def tile_controlvariateexp2linearbanditpolicy_x2_kernel(
             ln(i, slice(0, N) if c is None else slice(256 * c, 256 * c + 256))
 
         def w(b, c):
-            ncols = slice(256 * c, 256 * c + 256)
-            live["ob", b, c] = ob = work.tile([P, 256, 4], BF16, name="ob", tag="ob", bufs=4, align_bytes=64)
+            width = 512 if b == 0 else 256
+            ncols = slice(width * c, width * c + width)
+            live["ob", b, c] = ob = work.tile(
+                [P, width, 4], BF16, name="ob", tag="ob%d" % b, bufs=2 if b == 0 else 4, align_bytes=64
+            )
             src = o_sb[b][:, :, ncols].rearrange("p t n -> p n t")
             if "w%d%d" % (b, c) in GW:
                 nc.gpsimd.tensor_scalar(out=ob[:], in0=src, scalar1=1.0, scalar2=0.0, op0=ALU.mult, op1=ALU.add)
@@ -324,7 +364,8 @@ def tile_controlvariateexp2linearbanditpolicy_x2_kernel(
                 nc.vector.tensor_copy(out=ob[:], in_=src)
 
         def oq(b, c):
-            cols = slice(256 * c, 256 * c + 256)
+            width = 512 if b == 0 else 256
+            cols = slice(width * c, width * c + width)
             nc.vector.quantize_mx(
                 out=ocodes[b][:, cols].bitcast(FP8X4), scales=oscales[b][:, cols],
                 in_=live.pop(("ob", b, c))[:].rearrange("p n t -> p (n t)"),
@@ -340,7 +381,7 @@ def tile_controlvariateexp2linearbanditpolicy_x2_kernel(
                 )
 
         stages = {"VT": VT, "vc": vc, "vq": vq, "Z": Z, "z": z, "g": gm, "UT": UT, "uc": uc, "U": U, "u": u, "uq": uq, "S": S, "y": y,
-                  "e8": e8, "mx": mx_, "E": E, "q": q, "r": r, "l": l, "w": w, "oq": oq, "so": so,
+                  "e8": e8, "mx": mx_, "E": E, "q": q, "a": a, "b": b_, "Q": Q, "k": k, "l": l, "w": w, "oq": oq, "so": so,
                   "G": spread_g, "Gc": copy_g, "C": columns, "Cc": copy_columns, "M": spread_mu, "Mc": copy_mu, "c": scale_mu}
         for token in ORDER:
             name, digits = token.split(":")

@@ -23,15 +23,15 @@ NTILES = T // P
 SOFT = (0, 1, 2, 3, 4)
 MODE, NVT, NU, NZ, NS, GW, SW, GQ = "EE2B2B2B", 1, 2, 2, 3, ("w00", "w01"), ("w13",), ()
 ORDER = """
-VT:0 C: vc:0 G: Cc: vq:0 VT:1 Gc: Z:00 vc:1 Z:01 z:00 M: z:01 VT:2 Mc: vq:1 U:00 U:01 u:00 Z:10 vc:2 Z:11 u:01
-z:10 VT:3 z:11 vc:3 U:10 uq:0 vq:2 U:11 u:10 S:00 u:11 Z:21 Z:20 vq:3 y:00 k:21 S:01 uq:1 k:20 VT:4 c: U:21
-vc:4 y:01 U:20 u:21 Z:30 e8:0 vq:4 S:10 u:20 Z:31 z:30 S:11 uq:2 z:31 g:30 VT:5 mx:0 S:20 y:10 vc:5 g:31 Z:41
-y:11 E:0 Z:40 y:20 S:21 vq:5 k:40 UT:3 q:0 k:41 VT:6 uc:3 U:40 y:21 vc:6 Z:50 uq:3 e8:1 u:40 U:41 z:50 e8:2
-S:31 vq:6 u:41 S:30 g:50 Z:51 mx:1 y:31 E:1 VT:7 uq:4 z:51 Z:60 vc:7 y:30 S:40 g:51 Z:61 k:60 mx:2 y:40 S:41
-e8:3 vq:7 U:60 q:1 k:61 UT:5 E:2 u:60 Z:70 Z:71 mx:3 y:41 uc:5 z:70 E:3 z:71 U:61 g:70 e8:4 a:0 u:61 g:71 b:0
-mx:4 uq:5 uq:6 UT:7 q:2 l:0 S:51 S:60 q:3 uc:7 S:50 l:2 y:60 uq:7 l:3 y:50 S:71 y:51 l:1 S:61 y:71 S:70 mx:5
-w:00 y:61 y:70 E:4 mx:6 w:01 E:5 mx:7 E:6 oq:00 E:7 oq:01 so:0 a:1 q:4 b:1 a:2 q:6 l:4 b:2 q:5 l:6 q:7 l:5
-l:71 l:73 l:70 w:11 l:72 w:13 w:10 w:12 oq:11 oq:13 oq:10 oq:12 so:1
+VT:0 C: vc:0 G: Cc: vq:0 VT:1 Gc: Z:00 vc:1 Z:01 z:00 M: z:01 U:00 Mc: vq:1 VT:2 u:00 U:01 Z:10 vc:2 u:01 Z:11
+z:10 VT:3 z:11 U:10 vc:3 vq:2 uq:0 U:11 u:10 Z:21 vq:3 Z:20 u:11 k:21 S:00 c: k:20 S:01 U:21 uq:1 y:00 U:20
+y:01 VT:4 u:21 Z:30 u:20 vc:4 Z:31 e8:0 z:30 S:10 vq:4 VT:5 uq:2 z:31 g:30 Z:40 vc:5 mx:0 S:20 y:10 k:40 S:11
+g:31 y:20 E:0 Z:41 y:11 S:21 k:41 vq:5 UT:3 y:21 VT:6 q:0 uc:3 Z:51 vc:6 Z:50 uq:3 e8:1 U:40 z:51 z:50 VT:7
+e8:2 vq:6 U:41 mx:1 g:50 u:40 vc:7 S:31 u:41 E:1 S:30 g:51 mx:2 y:31 Z:60 Z:61 y:30 E:2 UT:5 uq:4 vq:7 k:60
+q:1 S:41 k:61 S:40 uc:5 y:41 Z:70 e8:3 Z:71 y:40 U:60 z:70 e8:4 uq:5 U:61 mx:3 g:70 z:71 S:50 E:3 u:60 S:51
+g:71 u:61 a:0 mx:4 uq:6 UT:7 b:0 y:50 S:60 l:0 q:2 S:61 uc:7 y:51 l:1 q:3 l:2 uq:7 y:60 S:70 y:61 l:3 S:71
+mx:5 w:01 y:71 mx:6 E:5 y:70 w:00 E:4 mx:7 E:6 q:4 E:7 oq:01 a:1 b:1 q:6 l:4 a:2 q:5 b:2 l:6 q:7 l:5 oq:00
+so:0 l:70 l:71 w:10 l:72 w:11 l:73 w:12 w:13 oq:10 oq:11 oq:12 oq:13 so:1
 """.split()
 
 
@@ -83,9 +83,9 @@ def tile_controlvariateexp2linearbanditpolicy_x2_kernel(
                 out=dst[:, :, part].bitcast(I32), in_=src.rearrange("b p n -> p b n")[:, :, part].bitcast(I32)
             )
 
-        def load_tile(dst, src, i):
+        def load_tiles(dst, src, i, n):
             rows_of = src[512 * (i // 4) : 512 * (i // 4) + 512, :].rearrange("(p t) d -> p t d", t=4)
-            nc.sync.dma_start(out=dst[i // 4][:, i % 4, :], in_=rows_of[:, i % 4, :])
+            nc.sync.dma_start(out=dst[i // 4][:, i % 4 : i % 4 + n, :], in_=rows_of[:, i % 4 : i % 4 + n, :])
 
         nc.vector.memset(rows[:], 0.0)
         for r, src in enumerate((g, surp, mu)):
@@ -95,27 +95,23 @@ def tile_controlvariateexp2linearbanditpolicy_x2_kernel(
         nc.vector.memset(asc[:].bitcast(I32), 0)
         make_identity(nc, ident[:])
         nc.vector.tensor_copy(out=ident_bf[:], in_=ident[:])
-        load_tile(v_sb, v, 0)
+        load_tiles(v_sb, v, 0, 1)
         load_words(pw, pinv_words, 0)
         load_scales(ps, pinv_scales)
-        load_tile(v_sb, v, 1)
+        load_tiles(v_sb, v, 1, 1)
         load_words(pw, pinv_words, 1)
-        load_tile(m_sb, m, 0)
-        load_tile(v_sb, v, 2)
-        load_tile(m_sb, m, 1)
-        load_tile(m_sb, m, 2)
+        load_tiles(m_sb, m, 0, 1)
+        load_tiles(m_sb, m, 1, 1)
+        load_tiles(v_sb, v, 2, 2)
         load_words(aw, arms_words, 0)
         load_words(aw, arms_words, 1)
         load_scales(asc, arms_scales)
-        load_tile(logw_sb, logw, 0)
-        load_tile(v_sb, v, 3)
-        load_tile(m_sb, m, 3)
-        load_tile(logw_sb, logw, 1)
-        for i in range(2, NTILES):
-            if i > 3:
-                load_tile(v_sb, v, i)
-                load_tile(m_sb, m, i)
-            load_tile(logw_sb, logw, i)
+        load_tiles(m_sb, m, 2, 2)
+        load_tiles(logw_sb, logw, 0, 2)
+        load_tiles(v_sb, v, 4, 4)
+        load_tiles(logw_sb, logw, 2, 2)
+        load_tiles(m_sb, m, 4, 4)
+        load_tiles(logw_sb, logw, 4, 4)
 
         def spread(row, h, tag):
             bank = psum.tile([P, 512], F32, name=tag, tag=tag, bufs={"z": NZ, "s": NS}[tag])
@@ -337,17 +333,23 @@ def tile_controlvariateexp2linearbanditpolicy_x2_kernel(
                     out=e, in0=c_all[:], scalar=esum[i // 4][:, i % 4 : i % 4 + 1], in1=e, op0=ALU.mult, op1=ALU.add
                 )
 
-        def ln(i, cols):
+        def store_rows(i, cols):
             b, t = i // 4, i % 4
-            nc.scalar.activation(out=o_sb[b][:, t, cols], in_=e_sb[b][:, t, cols], func=ACT.Ln,
-                scale=inv[b][:, t : t + 1])
             nc.sync.dma_start(
                 out=out_0[512 * b : 512 * b + 512, cols].rearrange("(p t) n -> p t n", t=4)[:, t, :],
                 in_=o_sb[b][:, t, cols],
             )
 
         def l(i, c=None):
-            ln(i, slice(0, N) if c is None else slice(256 * c, 256 * c + 256))
+            b, t = i // 4, i % 4
+            cols = slice(0, N) if c is None else slice(256 * c, 256 * c + 256)
+            nc.scalar.activation(
+                out=o_sb[b][:, t, cols], in_=e_sb[b][:, t, cols], func=ACT.Ln, scale=inv[b][:, t : t + 1]
+            )
+            if c is None:
+                store_rows(i, cols)
+            elif c % 2 == 1:
+                store_rows(i, slice(512 * (c // 2), 512 * (c // 2) + 512))
 
         def w(b, c):
             width = 512 if b == 0 else 256
@@ -370,8 +372,11 @@ def tile_controlvariateexp2linearbanditpolicy_x2_kernel(
                 out=ocodes[b][:, cols].bitcast(FP8X4), scales=oscales[b][:, cols],
                 in_=live.pop(("ob", b, c))[:].rearrange("p n t -> p (n t)"),
             )
+            if b == 1 and c % 2 == 0:
+                return
+            half = slice(512 * (c // (b + 1)), 512 * (c // (b + 1)) + 512)
             nc.sync.dma_start(
-                out=out_1[b].rearrange("p n t -> p (n t)").bitcast(I32)[:, cols], in_=ocodes[b][:, cols].bitcast(I32)
+                out=out_1[b].rearrange("p n t -> p (n t)").bitcast(I32)[:, half], in_=ocodes[b][:, half].bitcast(I32)
             )
 
         def so(b):

import math
from contextlib import ExitStack

import concourse.mybir as mybir
from concourse.masks import make_identity

F32 = mybir.dt.float32
BF16 = mybir.dt.bfloat16
I32 = mybir.dt.int32
U32 = mybir.dt.uint32
U8 = mybir.dt.uint8
FP8X4 = mybir.dt.float8_e4m3fn_x4
FP4X4 = mybir.dt.float4_e2m1fn_x4
ALU = mybir.AluOpType
ACT = mybir.ActivationFunctionType
AX = mybir.AxisListType

P = 128
T, D, N = 1024, 1024, 1024
ETA, KEEP, MIX = 0.8, 0.85, 0.15
FLOPS = 2 * T * D * D + 2 * T * D * N
NTILES = T // P
SOFT = (0, 1, 2, 3, 4)
MODE, NVT, NU, NZ, NS, GW, SW, GQ = "EE2B2B2B", 1, 2, 2, 3, ("w00", "w01"), ("w13",), ()
ORDER = """
VT:0 C: vc:0 G: Cc: vq:0 VT:1 Gc: Z:00 vc:1 Z:01 z:00 M: z:01 U:00 Mc: vq:1 VT:2 u:00 U:01 Z:10 vc:2 u:01 Z:11
z:10 VT:3 z:11 U:10 vc:3 vq:2 uq:0 U:11 u:10 Z:21 vq:3 Z:20 u:11 k:21 S:00 c: k:20 S:01 U:21 uq:1 y:00 U:20
y:01 VT:4 u:21 Z:30 u:20 vc:4 Z:31 e8:0 z:30 S:10 vq:4 VT:5 uq:2 z:31 g:30 Z:40 vc:5 mx:0 S:20 y:10 k:40 S:11
g:31 y:20 E:0 Z:41 y:11 S:21 k:41 vq:5 UT:3 y:21 VT:6 q:0 uc:3 Z:51 vc:6 Z:50 uq:3 e8:1 U:40 z:51 z:50 VT:7
e8:2 vq:6 U:41 mx:1 g:50 u:40 vc:7 S:31 u:41 E:1 S:30 g:51 mx:2 y:31 Z:60 Z:61 y:30 E:2 UT:5 uq:4 vq:7 k:60
q:1 S:41 k:61 S:40 uc:5 y:41 Z:70 e8:3 Z:71 y:40 U:60 z:70 e8:4 uq:5 U:61 mx:3 g:70 z:71 S:50 E:3 u:60 S:51
g:71 u:61 a:0 mx:4 uq:6 UT:7 b:0 y:50 S:60 l:0 q:2 S:61 uc:7 y:51 l:1 q:3 l:2 uq:7 y:60 S:70 y:61 l:3 S:71
mx:5 w:01 y:71 mx:6 E:5 y:70 w:00 E:4 mx:7 E:6 q:4 E:7 oq:01 a:1 b:1 q:6 l:4 a:2 q:5 b:2 l:6 q:7 l:5 oq:00
so:0 l:70 l:71 w:10 l:72 w:11 l:73 w:12 w:13 oq:10 oq:11 oq:12 oq:13 so:1
""".split()


def tile_controlvariateexp2linearbanditpolicy_x2_kernel(
    tc, v, pinv_words, pinv_scales, surp, m, g, arms_words, arms_scales, logw, mu, out_0, out_1, out_2
):
    nc = tc.nc
    with ExitStack() as ctx:
        keep = ctx.enter_context(tc.tile_pool(name="keep", bufs=1))
        work = ctx.enter_context(tc.tile_pool(name="work", bufs=3))
        psum = ctx.enter_context(tc.psum_pool(name="psum", bufs=1))
        ctx.enter_context(tc.manual_schedule())

        v_sb = [keep.tile([P, 4, D], BF16, name="v_sb%d" % i, align_bytes=64) for i in range(2)]
        m_sb = [keep.tile([P, 4, D], BF16, name="m_sb%d" % i, align_bytes=64) for i in range(2)]
        logw_sb = [keep.tile([P, 4, N], BF16, name="logw_sb%d" % i, align_bytes=64) for i in range(2)]
        e_sb = [keep.tile([P, 4, N], F32, name="e_sb%d" % i, align_bytes=64) for i in range(2)]
        o_sb = [keep.tile([P, 4, N], F32, name="o_sb%d" % i, align_bytes=64) for i in range(2)]
        ocodes = [keep.tile([P, N], U32, name="ocodes%d" % i, align_bytes=64) for i in range(2)]
        oscales = [keep.tile([P, N], U8, name="oscales%d" % i, align_bytes=64) for i in range(2)]
        pw = keep.tile([P, 2, 2 * D], U8, name="pw", align_bytes=64)
        aw = keep.tile([P, 2, 2 * N], U8, name="aw", align_bytes=64)
        ps = keep.tile([P, 2 * D], U8, name="ps", align_bytes=64)
        asc = keep.tile([P, 2 * N], U8, name="asc", align_bytes=64)
        cols = keep.tile([P, 2, NTILES], F32, name="cols")
        g_all = keep.tile([P, D], BF16, name="g_all", align_bytes=64)
        rows = keep.tile([P, D], BF16, name="rows", align_bytes=64)
        ident = keep.tile([P, P], F32, name="ident", align_bytes=64)
        ident_bf = keep.tile([P, P], BF16, name="ident_bf", align_bytes=64)
        c_all = keep.tile([P, N], F32, name="c_all", align_bytes=64)
        mu_sum = keep.tile([P, 2], F32, name="mu_sum")
        mu_rec = keep.tile([P, 1], F32, name="mu_rec")
        warm = keep.tile([P, 1], F32, name="warm")
        esum = [keep.tile([P, 4], F32, name="esum%d" % i) for i in range(2)]
        inv = [keep.tile([P, 4], F32, name="inv%d" % i) for i in range(2)]
        shift = [keep.tile([P, 1], F32, name="shift%d" % i) for i in range(NTILES)]
        soft = [keep.tile([P, 1], F32, name="soft%d" % i) for i in range(NTILES)]

        def load_scales(dst, src):
            for q in range(4):
                nc.sync.dma_start(
                    out=dst[32 * q : 32 * q + 4, :].bitcast(I32).rearrange("r (b n) -> r b n", b=2),
                    in_=src[:, 4 * q : 4 * q + 4, :].rearrange("b r n -> r b n").bitcast(I32),
                )

        def load_words(dst, src, h):
            part = slice(D * h, D * h + D)
            nc.sync.dma_start(
                out=dst[:, :, part].bitcast(I32), in_=src.rearrange("b p n -> p b n")[:, :, part].bitcast(I32)
            )

        def load_tiles(dst, src, i, n):
            rows_of = src[512 * (i // 4) : 512 * (i // 4) + 512, :].rearrange("(p t) d -> p t d", t=4)
            nc.sync.dma_start(out=dst[i // 4][:, i % 4 : i % 4 + n, :], in_=rows_of[:, i % 4 : i % 4 + n, :])

        nc.vector.memset(rows[:], 0.0)
        for r, src in enumerate((g, surp, mu)):
            nc.scalar.dma_start(out=rows[r : r + 1, :], in_=src.rearrange("(o d) -> o d", o=1))
        nc.scalar.activation(out=warm[:], in_=warm_src(nc, keep), func=ACT.Exp)
        nc.vector.memset(ps[:].bitcast(I32), 0)
        nc.vector.memset(asc[:].bitcast(I32), 0)
        make_identity(nc, ident[:])
        nc.vector.tensor_copy(out=ident_bf[:], in_=ident[:])
        load_tiles(v_sb, v, 0, 1)
        load_words(pw, pinv_words, 0)
        load_scales(ps, pinv_scales)
        load_tiles(v_sb, v, 1, 1)
        load_words(pw, pinv_words, 1)
        load_tiles(m_sb, m, 0, 1)
        load_tiles(m_sb, m, 1, 1)
        load_tiles(v_sb, v, 2, 2)
        load_words(aw, arms_words, 0)
        load_words(aw, arms_words, 1)
        load_scales(asc, arms_scales)
        load_tiles(m_sb, m, 2, 2)
        load_tiles(logw_sb, logw, 0, 2)
        load_tiles(v_sb, v, 4, 4)
        load_tiles(logw_sb, logw, 2, 2)
        load_tiles(m_sb, m, 4, 4)
        load_tiles(logw_sb, logw, 4, 4)

        def spread(row, h, tag):
            bank = psum.tile([P, 512], F32, name=tag, tag=tag, bufs={"z": NZ, "s": NS}[tag])
            nc.tensor.matmul(
                bank[:], lhsT=ident_bf[:, row : row + 1].to_broadcast([P, P]), rhs=rows[:, 512 * h : 512 * h + 512],
                start=True, stop=True,
            )
            return bank

        def columns():
            live["cols"] = bank = psum.tile([P, 512], F32, name="s", tag="s", bufs=NS)
            for i in range(NTILES):
                first = 512 * (i // 4) + i % 4
                nc.tensor.matmul(
                    bank[:, 2 * i : 2 * i + 2], lhsT=rows[:, first : first + 509 : 4], rhs=ident_bf[:, 0:2],
                    start=True, stop=True,
                )

        def copy_columns():
            bank = live.pop("cols")
            nc.vector.tensor_copy(out=cols[:], in_=bank[:, 0 : 2 * NTILES].rearrange("p (i r) -> p r i", r=2))

        def spread_g():
            for h in range(2):
                live["g", h] = spread(0, h, "z")

        def copy_g():
            for h in range(2):
                nc.vector.tensor_copy(out=g_all[:, 512 * h : 512 * h + 512], in_=live.pop(("g", h))[:])

        def spread_mu():
            for h in range(2):
                live["mu", h] = spread(2, h, "s")

        def copy_mu():
            for h in range(2):
                bank = live.pop(("mu", h))
                nc.scalar.activation(
                    out=c_all[:, 512 * h : 512 * h + 512], in_=bank[:], func=ACT.Identity,
                    accum_out=mu_sum[:, h : h + 1],
                )

        def scale_mu():
            nc.vector.tensor_add(out=mu_rec[:], in0=mu_sum[:, 0:1], in1=mu_sum[:, 1:2])
            nc.vector.reciprocal(out=mu_rec[:], in_=mu_rec[:])
            nc.vector.tensor_scalar(
                out=c_all[:], in0=c_all[:], scalar1=mu_rec[:], scalar2=MIX / KEEP, op0=ALU.mult, op1=ALU.mult
            )

        live = {}

        def transposes(src, bank):
            words = src.bitcast(F32)
            for b in range(2):
                for u in range(2):
                    nc.tensor.transpose(
                        bank[:, b, u, :], words[:, 256 * b + u : 256 * (b + 1) : 2], ident[:]
                    )

        def words_out(bank, name):
            kt = work.tile([P, 2 * P * 4], BF16, name=name, tag=name, align_bytes=64)
            nc.scalar.copy(
                out=kt[:].bitcast(F32).rearrange("p (b r u) -> p b r u", b=2, u=2),
                in_=bank[:].rearrange("p b u r -> p b r u"),
            )
            return kt

        def quantize(src, name, bufs):
            codes = work.tile([P, 2 * P], U32, name=name + "c", tag=name + "c", bufs=bufs, align_bytes=64)
            scales = work.tile([P, 2 * P], U8, name=name + "s", tag=name + "s", bufs=bufs, align_bytes=64)
            nc.vector.quantize_mx(out=codes[:].bitcast(FP8X4), scales=scales[:], in_=src)
            return codes, scales

        def mx(bank, act, words, scales, h):
            codes, act_scales = act
            for b in range(2):
                nc.tensor.matmul_mx(
                    out=bank[:],
                    lhsT=codes[:, P * b : P * b + P].bitcast(FP8X4),
                    lhsT_scale=act_scales[:, P * b : P * b + P],
                    rhs=words[:, b, 1024 * h : 1024 * h + 1024].bitcast(FP4X4),
                    rhs_scale=scales[:, 1024 * b + 512 * h : 1024 * b + 512 * h + 512],
                    start=(b == 0),
                    stop=(b == 1),
                )

        def VT(i):
            live["vtp", i] = bank = psum.tile([P, 2, 2, P], F32, name="vtp", tag="vtp", bufs=NVT)
            transposes(v_sb[i // 4][:, i % 4, :], bank)

        def vc(i):
            live["vt", i] = words_out(live.pop(("vtp", i)), "vt")

        def vq(i):
            live["vx", i] = quantize(live.pop(("vt", i))[:], "vx", 5)

        def Z(i, h):
            live["z", i, h] = bank = psum.tile([P, 512], F32, name="z", tag="z", bufs=NZ)
            mx(bank, live["vx", i], pw, ps, h)

        def z(i, h):
            if ("lh", i) not in live:
                live["lh", i] = work.tile([P, 2, 512], F32, name="lh", tag="lh", bufs=5, align_bytes=64)
            out, src = live["lh", i][:, h, :], live.pop(("z", i, h))[:]
            other = m_sb[i // 4][:, i % 4, 512 * h : 512 * h + 512]
            if MODE[i] == "E":
                out = out.rearrange("p (t j) -> p t j", t=4)
                src, other = (x.rearrange("p (j t) -> p t j", t=4) for x in (src, other))
            nc.vector.scalar_tensor_tensor(
                out=out, in0=src, scalar=cols[:, 1, i : i + 1], in1=other, op0=ALU.mult, op1=ALU.add
            )

        def k(i, h):
            if ("lh", i) not in live:
                live["lh", i] = work.tile([P, 2, 512], F32, name="lh", tag="lh", bufs=5, align_bytes=64)
            nc.scalar.activation(
                out=live["lh", i][:, h, :].rearrange("p (t j) -> p t j", t=4),
                in_=live.pop(("z", i, h))[:].rearrange("p (j t) -> p t j", t=4), func=ACT.Copy,
                scale=cols[:, 1, i : i + 1],
            )

        def gm(i, h):
            if ("u", i) not in live:
                live["u", i] = work.tile([P, D], BF16, name="u", tag="u", bufs=5, align_bytes=64)
            part = slice(512 * h, 512 * h + 512)
            nc.gpsimd.tensor_tensor(
                out=live["u", i][:, part], in0=live["lh", i][:, h, :], in1=g_all[:, part], op=ALU.mult
            )

        def UT(i):
            live["utp", i] = bank = psum.tile([P, 2, 2, P], F32, name="up", tag="up", bufs=NU)
            transposes(live.pop(("u", i))[:], bank)

        def uc(i):
            live["ut", i] = words_out(live.pop(("utp", i)), "ut")

        def U(i, h):
            live["U", i, h] = bank = psum.tile([P, 4, P], F32, name="up", tag="up", bufs=NU)
            for t in range(4):
                part = live["lh", i][:, h, P * t : P * t + P]
                if MODE[i] == "E":
                    nc.tensor.transpose(bank[:, t, :], part, ident[:])
                else:
                    nc.tensor.matmul(
                        bank[:, t, :], lhsT=m_sb[i // 4][:, i % 4, 512 * h + t : 512 * h + t + 509 : 4],
                        rhs=ident_bf[:], start=True, stop=False,
                    )
                    nc.tensor.matmul(
                        bank[:, t, :], lhsT=part, rhs=ident[:], is_transpose=True, start=False, stop=True
                    )

        def u(i, h):
            if ("ut", i) not in live:
                live["ut", i] = work.tile([P, 2 * P * 4], BF16, name="ut", tag="ut", align_bytes=64)
            nc.vector.tensor_tensor(
                out=live["ut", i][:, 512 * h : 512 * h + 512].rearrange("p (r t) -> p r t", t=4),
                in0=live.pop(("U", i, h))[:].rearrange("p t r -> p r t"),
                in1=cols[:, 0:1, 4 * h : 4 * h + 4].to_broadcast([P, P, 4]), op=ALU.mult,
            )

        def uq(i):
            live["ux", i] = quantize(live.pop(("ut", i))[:], "ux", 4)

        def S(i, h):
            live["s", i, h] = bank = psum.tile([P, 512], F32, name="s", tag="s", bufs=NS)
            mx(bank, live["ux", i], aw, asc, h)

        def y(i, h):
            if ("y", i) not in live:
                live["y", i] = work.tile([P, N], F32, name="y", tag="y", bufs=4, align_bytes=64)
            cols = slice(512 * h, 512 * h + 512)
            nc.vector.scalar_tensor_tensor(
                out=live["y", i][:, cols], in0=live.pop(("s", i, h))[:], scalar=ETA,
                in1=logw_sb[i // 4][:, i % 4, cols], op0=ALU.mult, op1=ALU.subtract,
            )

        def e8(i):
            junk = work.tile([P, N], BF16, name="junk", tag="junk", bufs=2, align_bytes=64)
            nc.scalar.activation(out=junk[:], in_=live["y", i][:], func=ACT.Exp, scale=-0.125, accum_out=soft[i][:])

        def mx_(i):
            if i in SOFT:
                nc.vector.tensor_scalar(
                    out=shift[i][:], in0=soft[i][:].bitcast(I32), scalar1=-8.0 * math.log(2.0) / 2.0**23,
                    scalar2=8.0 * 127.0 * math.log(2.0), op0=ALU.mult, op1=ALU.add,
                )
            else:
                nc.vector.tensor_reduce(out=shift[i][:], in_=live["y", i][:], axis=AX.X, op=ALU.min)

        def E(i):
            nc.scalar.activation(
                out=e_sb[i // 4][:, i % 4, :], in_=live.pop(("y", i))[:], func=ACT.Exp, scale=-1.0,
                bias=shift[i][:], accum_out=esum[i // 4][:, i % 4 : i % 4 + 1],
            )

        RANGES = [(0, slice(0, 4)), (1, slice(0, 3)), (1, slice(3, 4))]

        def a(k):
            b, part = RANGES[k]
            nc.vector.tensor_scalar_mul(out=inv[b][:, part], in0=esum[b][:, part], scalar1=1.0 / (KEEP * N))

        def b_(k):
            b, part = RANGES[k]
            nc.vector.reciprocal(out=inv[b][:, part], in_=inv[b][:, part])

        def Q(i):
            live["cs", i] = cs = work.tile([P, N], F32, name="cs", tag="cs", bufs=1, align_bytes=64)
            nc.gpsimd.tensor_scalar(
                out=cs[:], in0=c_all[:], scalar1=esum[i // 4][:, i % 4 : i % 4 + 1], scalar2=0.0, op0=ALU.mult,
                op1=ALU.add,
            )

        def q(i):
            e = e_sb[i // 4][:, i % 4, :]
            if i in GQ:
                nc.gpsimd.tensor_tensor(out=e, in0=e, in1=live.pop(("cs", i))[:], op=ALU.add)
            else:
                nc.vector.scalar_tensor_tensor(
                    out=e, in0=c_all[:], scalar=esum[i // 4][:, i % 4 : i % 4 + 1], in1=e, op0=ALU.mult, op1=ALU.add
                )

        def store_rows(i, cols):
            b, t = i // 4, i % 4
            nc.sync.dma_start(
                out=out_0[512 * b : 512 * b + 512, cols].rearrange("(p t) n -> p t n", t=4)[:, t, :],
                in_=o_sb[b][:, t, cols],
            )

        def l(i, c=None):
            b, t = i // 4, i % 4
            cols = slice(0, N) if c is None else slice(256 * c, 256 * c + 256)
            nc.scalar.activation(
                out=o_sb[b][:, t, cols], in_=e_sb[b][:, t, cols], func=ACT.Ln, scale=inv[b][:, t : t + 1]
            )
            if c is None:
                store_rows(i, cols)
            elif c % 2 == 1:
                store_rows(i, slice(512 * (c // 2), 512 * (c // 2) + 512))

        def w(b, c):
            width = 512 if b == 0 else 256
            ncols = slice(width * c, width * c + width)
            live["ob", b, c] = ob = work.tile(
                [P, width, 4], BF16, name="ob", tag="ob%d" % b, bufs=2 if b == 0 else 4, align_bytes=64
            )
            src = o_sb[b][:, :, ncols].rearrange("p t n -> p n t")
            if "w%d%d" % (b, c) in GW:
                nc.gpsimd.tensor_scalar(out=ob[:], in0=src, scalar1=1.0, scalar2=0.0, op0=ALU.mult, op1=ALU.add)
            elif "w%d%d" % (b, c) in SW:
                nc.scalar.copy(out=ob[:], in_=src)
            else:
                nc.vector.tensor_copy(out=ob[:], in_=src)

        def oq(b, c):
            width = 512 if b == 0 else 256
            cols = slice(width * c, width * c + width)
            nc.vector.quantize_mx(
                out=ocodes[b][:, cols].bitcast(FP8X4), scales=oscales[b][:, cols],
                in_=live.pop(("ob", b, c))[:].rearrange("p n t -> p (n t)"),
            )
            if b == 1 and c % 2 == 0:
                return
            half = slice(512 * (c // (b + 1)), 512 * (c // (b + 1)) + 512)
            nc.sync.dma_start(
                out=out_1[b].rearrange("p n t -> p (n t)").bitcast(I32)[:, half], in_=ocodes[b][:, half].bitcast(I32)
            )

        def so(b):
            for r in range(4):
                nc.sync.dma_start(
                    out=out_2[b][4 * r : 4 * r + 4, :].bitcast(I32), in_=oscales[b][32 * r : 32 * r + 4, :].bitcast(I32)
                )

        stages = {"VT": VT, "vc": vc, "vq": vq, "Z": Z, "z": z, "g": gm, "UT": UT, "uc": uc, "U": U, "u": u, "uq": uq, "S": S, "y": y,
                  "e8": e8, "mx": mx_, "E": E, "q": q, "a": a, "b": b_, "Q": Q, "k": k, "l": l, "w": w, "oq": oq, "so": so,
                  "G": spread_g, "Gc": copy_g, "C": columns, "Cc": copy_columns, "M": spread_mu, "Mc": copy_mu, "c": scale_mu}
        for token in ORDER:
            name, digits = token.split(":")
            stages[name](*[int(x) for x in digits])


def warm_src(nc, keep):
    one = keep.tile([P, 1], F32, name="one")
    nc.vector.memset(one[:], 1.0)
    return one[:]
